import numpy as np
import ml_dtypes


def mxq(x, axis, fmt="e4m3"):
    dtype, down = {"e4m3": (ml_dtypes.float8_e4m3fn, 7), "e5m2": (ml_dtypes.float8_e5m2, 14)}[fmt]
    v = np.moveaxis(np.asarray(x, np.float32).astype(ml_dtypes.bfloat16).astype(np.float64), axis, -1)
    blocks = v.reshape(v.shape[:-1] + (-1, 32))
    amax = np.abs(blocks).max(-1, keepdims=True)
    byte = np.maximum(np.where(amax > 0, np.frexp(amax)[1] - 1 + 127, 0) - down, 1)
    scale = np.exp2(byte - 127.0)
    codes = (blocks / scale).astype(np.float32).astype(dtype).astype(np.float64)
    return np.moveaxis((codes * scale).reshape(v.shape), -1, axis)


WIDE = False


def mx_kscale(k):
    if not WIDE:
        return np.ones(k)
    levels = np.array([10, -10, 5, -5, 0])
    if k % 512:
        return np.exp2(np.random.permutation(np.resize(levels, k // 32))).repeat(32)
    a = np.empty((k // 512, 16))
    for p in range(k // 512):
        a[p, :8] = np.random.permutation(np.resize(levels, 8))
        for g in range(8):
            far = levels[np.abs(levels - a[p, g]) >= 10]
            a[p, g + 8] = far[np.random.randint(len(far))]
    return np.exp2(a.ravel()).repeat(32)


def f64(x):
    return np.asarray(x).astype(np.float64)


def striped(idx):
    return np.tile(np.asarray(idx).reshape(-1, 16).T, (8, 1)).astype(np.uint16)


def unstriped(offs):
    return offs[:16].T.reshape(-1).astype(np.int64)


G, K, T, D, M = 256, 4, 2048, 512, 256


def setup_inputs():
    n = np.random.standard_normal
    s = mx_kscale(D)[:, None]
    x = n((D, T)) * s
    idx = np.stack([np.random.permutation(T)[:K] for g in range(G)])
    return {
        "xT": x.astype(np.float32),
        "w": (n((D, M)) / np.sqrt(D) / s).astype(np.float32),
        "bias": (n((M, 1)) - 2.0).astype(np.float32),
        "offs": striped(idx.reshape(-1)),
    }


def reference(xT, w, bias, offs):
    x = f64(xT)[:, unstriped(offs)]
    y = (mxq(f64(w), 0, "e4m3").T @ mxq(x, 0, "e4m3")).reshape(M, G, K).max(-1)
    y = y + f64(bias)
    y = np.maximum(y, 0.0)
    return y

@@ -1,0 +1,165 @@
+from contextlib import ExitStack
+
+import concourse.mybir as mybir
+from concourse.masks import make_identity
+
+G, K, T, D, M = 256, 4, 2048, 512, 256
+FLOPS = 2 * D * M * G * K
+
+P = 128
+PACK = 4
+E = 256
+CHUNKS = [(0, 256), (256, 256), (512, 256), (768, 128), (896, 128)]
+NS = len(CHUNKS)
+MB = M // P
+
+F32 = mybir.dt.float32
+BF16 = mybir.dt.bfloat16
+U32 = mybir.dt.uint32
+U16 = mybir.dt.uint16
+U8 = mybir.dt.uint8
+FP8X4 = mybir.dt.float8_e4m3fn_x4
+MAX = mybir.AluOpType.max
+MULT = mybir.AluOpType.mult
+ADD = mybir.AluOpType.add
+RELU = mybir.ActivationFunctionType.Relu
+X = mybir.AxisListType.X
+
+
+def tile_attend_edge_relu_kernel(tc, xT, w, bias, offs, out):
+    nc = tc.nc
+    with ExitStack() as ctx:
+        keep = ctx.enter_context(tc.tile_pool(name="keep", bufs=1))
+        psum = ctx.enter_context(tc.psum_pool(name="psum", bufs=1))
+
+        offsets = keep.tile([P, G * K // 16], U16, name="offsets")
+        nc.sync.dma_start(offsets[:], offs)
+
+        x_rows = xT.rearrange("(p t) c -> p t c", t=PACK)
+        planes = []
+        for t in range(PACK):
+            plane = keep.tile([P, T], F32, name="plane%d" % t, align_bytes=64)
+            nc.sync.dma_start(plane[:], x_rows[:, t, :])
+            planes.append(plane)
+        w_raw = keep.tile([P, PACK, M], F32, name="w_raw", align_bytes=64)
+        nc.sync.dma_start(w_raw[:], w.rearrange("(p t) m -> p t m", t=PACK))
+        bias_sb = []
+        for m in range(MB):
+            b = keep.tile([P, 1], F32, name="bias%d" % m)
+            nc.sync.dma_start(b[:], bias[m * P : (m + 1) * P, :])
+            bias_sb.append(b)
+
+        warm = keep.tile([P, 1], F32, name="warm")
+        nc.gpsimd.memset(warm[:], 0.0)
+        nc.scalar.activation(warm[:], warm[:], RELU)
+
+        g01 = keep.tile([P, 2, G * K], F32, name="g01", align_bytes=64)
+        g23 = keep.tile([P, 2, G * K], F32, name="g23", align_bytes=64)
+        xb = [keep.tile([P, n, PACK], BF16, name="xb%d" % s, align_bytes=64) for s, (c, n) in enumerate(CHUNKS)]
+        codes = [keep.tile([P, n], U32, name="codes%d" % s, align_bytes=64) for s, (c, n) in enumerate(CHUNKS)]
+        scales = [keep.tile([P, n], U8, name="scales%d" % s, align_bytes=64) for s, (c, n) in enumerate(CHUNKS)]
+        wb = keep.tile([P, M, PACK], BF16, name="wb", align_bytes=64)
+        w_codes = keep.tile([P, M], U32, name="w_codes", align_bytes=64)
+        w_scales = keep.tile([P, M], U8, name="w_scales", align_bytes=64)
+        acc = [psum.tile([P, MB, n], F32, name="acc%d" % s) for s, (c, n) in enumerate(CHUNKS)]
+        turned = psum.tile([P, 4, P], BF16, name="turned")
+        ident = keep.tile([P, P], BF16, name="ident")
+        make_identity(nc, ident[:])
+        best = keep.tile([P, MB, G], F32, name="best")
+        res = keep.tile([P, MB, G], F32, name="res")
+
+        def gather(t, first, count):
+            dst = g01 if t < 2 else g23
+            nc.vector.tensor_copy(
+                dst[:, t % 2, first : first + count],
+                planes[t][:].indirect(offsets[:, first // 16 : (first + count) // 16]),
+            )
+
+        def interleave(src, t0, s):
+            nc.scalar.copy(
+                xb[s][:, :, t0 : t0 + 2],
+                src[:, :, CHUNKS[s][0] : CHUNKS[s][0] + CHUNKS[s][1]].rearrange("p t n -> p n t"),
+            )
+
+        def quantise(s):
+            nc.vector.quantize_mx(
+                out=codes[s][:].bitcast(FP8X4),
+                scales=scales[s][:],
+                in_=xb[s][:].rearrange("p n t -> p (n t)"),
+            )
+
+        def multiply(s):
+            for m in range(MB):
+                nc.tensor.matmul_mx(
+                    out=acc[s][:, m, :],
+                    lhsT=w_codes[:, m * P : (m + 1) * P].bitcast(FP8X4),
+                    lhsT_scale=w_scales[:, m * P : (m + 1) * P],
+                    rhs=codes[s][:].bitcast(FP8X4),
+                    rhs_scale=scales[s][:],
+                    start=True,
+                    stop=True,
+                )
+
+        def reduce(s):
+            nc.vector.tensor_reduce(
+                out=best[:, :, CHUNKS[s][0] // K : (CHUNKS[s][0] + CHUNKS[s][1]) // K],
+                in_=acc[s][:].rearrange("p m (g j) -> p m g j", j=K),
+                axis=X,
+                op=MAX,
+            )
+
+        def finish(first, count):
+            for m in range(MB):
+                nc.scalar.activation(
+                    res[:, m, first : first + count], best[:, m, first : first + count], RELU, bias=bias_sb[m][:, 0:1]
+                )
+            nc.sync.dma_start(
+                out.rearrange("(m p) g -> p m g", p=P)[:, :, first : first + count], res[:, :, first : first + count]
+            )
+
+        for t in range(3):
+            for h in range(2):
+                gather(t, h * 2 * E, 2 * E)
+            if t == 1:
+                for s in range(NS):
+                    interleave(g01, 0, s)
+        for q in range(4):
+            nc.gpsimd.tensor_scalar(
+                wb[:, q * 64 : (q + 1) * 64, :],
+                w_raw[:, :, q * 64 : (q + 1) * 64].rearrange("p t m -> p m t"),
+                1.0, 0.0, MULT, ADD,
+            )
+        gather(3, 0, E)
+        interleave(g23, 2, 0)
+        gather(3, E, E)
+        interleave(g23, 2, 1)
+        for q in range(12):
+            c = q % 8 * 32
+            nc.tensor.transpose(
+                turned[:, q % 4, :], xb[0][:, c : c + 32, :].rearrange("p n t -> p (n t)"), ident[:]
+            )
+        gather(3, 2 * E, E)
+        interleave(g23, 2, 2)
+        quantise(0)
+        nc.vector.quantize_mx(
+            out=w_codes[:].bitcast(FP8X4), scales=w_scales[:], in_=wb[:].rearrange("p m t -> p (m t)")
+        )
+        multiply(0)
+        gather(3, 3 * E, E)
+        interleave(g23, 2, 3)
+        interleave(g23, 2, 4)
+        quantise(1)
+        multiply(1)
+        reduce(0)
+        quantise(2)
+        multiply(2)
+        reduce(1)
+        finish(0, 128)
+        quantise(3)
+        multiply(3)
+        reduce(2)
+        quantise(4)
+        multiply(4)
+        reduce(3)
+        reduce(4)
+        finish(128, 128)

@@ -8,9 +8,10 @@ FLOPS = 2 * D * M * G * K
 
 P = 128
 PACK = 4
-E = 256
-CHUNKS = [(0, 256), (256, 256), (512, 256), (768, 128), (896, 128)]
-NS = len(CHUNKS)
+NH = 2
+HE = G * K // NH
+HG = G // NH
+B = 256
 MB = M // P
 
 F32 = mybir.dt.float32
@@ -52,21 +53,18 @@ def tile_attend_edge_relu_kernel(tc, xT, w, bias, offs, out):
         warm = keep.tile([P, 1], F32, name="warm")
         nc.gpsimd.memset(warm[:], 0.0)
         nc.scalar.activation(warm[:], warm[:], RELU)
+        ident = keep.tile([P, P], BF16, name="ident")
+        make_identity(nc, ident[:])
 
         g01 = keep.tile([P, 2, G * K], F32, name="g01", align_bytes=64)
         g23 = keep.tile([P, 2, G * K], F32, name="g23", align_bytes=64)
-        xb = [keep.tile([P, n, PACK], BF16, name="xb%d" % s, align_bytes=64) for s, (c, n) in enumerate(CHUNKS)]
-        codes = [keep.tile([P, n], U32, name="codes%d" % s, align_bytes=64) for s, (c, n) in enumerate(CHUNKS)]
-        scales = [keep.tile([P, n], U8, name="scales%d" % s, align_bytes=64) for s, (c, n) in enumerate(CHUNKS)]
+        xb = [keep.tile([P, HE, PACK], BF16, name="xb%d" % h, align_bytes=64) for h in range(NH)]
+        codes = [keep.tile([P, HE], U32, name="codes%d" % h, align_bytes=64) for h in range(NH)]
+        scales = [keep.tile([P, HE], U8, name="scales%d" % h, align_bytes=64) for h in range(NH)]
         wb = keep.tile([P, M, PACK], BF16, name="wb", align_bytes=64)
         w_codes = keep.tile([P, M], U32, name="w_codes", align_bytes=64)
         w_scales = keep.tile([P, M], U8, name="w_scales", align_bytes=64)
-        acc = [psum.tile([P, MB, n], F32, name="acc%d" % s) for s, (c, n) in enumerate(CHUNKS)]
         turned = psum.tile([P, 4, P], BF16, name="turned")
-        ident = keep.tile([P, P], BF16, name="ident")
-        make_identity(nc, ident[:])
-        best = keep.tile([P, MB, G], F32, name="best")
-        res = keep.tile([P, MB, G], F32, name="res")
 
         def gather(t, first, count):
             dst = g01 if t < 2 else g23
@@ -76,52 +74,46 @@ def tile_attend_edge_relu_kernel(tc, xT, w, bias, offs, out):
             )
 
         def interleave(src, t0, s):
+            h, c = divmod(s * B, HE)
             nc.scalar.copy(
-                xb[s][:, :, t0 : t0 + 2],
-                src[:, :, CHUNKS[s][0] : CHUNKS[s][0] + CHUNKS[s][1]].rearrange("p t n -> p n t"),
+                xb[h][:, c : c + B, t0 : t0 + 2],
+                src[:, :, s * B : (s + 1) * B].rearrange("p t n -> p n t"),
             )
 
-        def quantise(s):
+        def quantise(h):
             nc.vector.quantize_mx(
-                out=codes[s][:].bitcast(FP8X4),
-                scales=scales[s][:],
-                in_=xb[s][:].rearrange("p n t -> p (n t)"),
+                out=codes[h][:].bitcast(FP8X4),
+                scales=scales[h][:],
+                in_=xb[h][:].rearrange("p n t -> p (n t)"),
             )
 
-        def multiply(s):
-            for m in range(MB):
-                nc.tensor.matmul_mx(
-                    out=acc[s][:, m, :],
-                    lhsT=w_codes[:, m * P : (m + 1) * P].bitcast(FP8X4),
-                    lhsT_scale=w_scales[:, m * P : (m + 1) * P],
-                    rhs=codes[s][:].bitcast(FP8X4),
-                    rhs_scale=scales[s][:],
-                    start=True,
-                    stop=True,
-                )
+        def multiply(h, m):
+            acc = psum.tile([P, HE], F32, name="acc%d%d" % (h, m))
+            nc.tensor.matmul_mx(
+                out=acc[:],
+                lhsT=w_codes[:, m * P : (m + 1) * P].bitcast(FP8X4),
+                lhsT_scale=w_scales[:, m * P : (m + 1) * P],
+                rhs=codes[h][:].bitcast(FP8X4),
+                rhs_scale=scales[h][:],
+                start=True,
+                stop=True,
+            )
+            return acc
 
-        def reduce(s):
+        def finish(h, m, acc):
+            best = keep.tile([P, HG], F32, name="best%d%d" % (h, m))
+            res = keep.tile([P, HG], F32, name="res%d%d" % (h, m))
             nc.vector.tensor_reduce(
-                out=best[:, :, CHUNKS[s][0] // K : (CHUNKS[s][0] + CHUNKS[s][1]) // K],
-                in_=acc[s][:].rearrange("p m (g j) -> p m g j", j=K),
-                axis=X,
-                op=MAX,
+                out=best[:], in_=acc[:].rearrange("p (g j) -> p g j", j=K), axis=X, op=MAX
             )
-
-        def finish(first, count):
-            for m in range(MB):
-                nc.scalar.activation(
-                    res[:, m, first : first + count], best[:, m, first : first + count], RELU, bias=bias_sb[m][:, 0:1]
-                )
-            nc.sync.dma_start(
-                out.rearrange("(m p) g -> p m g", p=P)[:, :, first : first + count], res[:, :, first : first + count]
-            )
+            nc.scalar.activation(res[:], best[:], RELU, bias=bias_sb[m][:, 0:1])
+            nc.sync.dma_start(out[m * P : (m + 1) * P, h * HG : (h + 1) * HG], res[:])
 
         for t in range(3):
-            for h in range(2):
-                gather(t, h * 2 * E, 2 * E)
+            for h in range(NH):
+                gather(t, h * HE, HE)
             if t == 1:
-                for s in range(NS):
+                for s in range(4):
                     interleave(g01, 0, s)
         for q in range(4):
             nc.gpsimd.tensor_scalar(
@@ -129,37 +121,29 @@ def tile_attend_edge_relu_kernel(tc, xT, w, bias, offs, out):
                 w_raw[:, :, q * 64 : (q + 1) * 64].rearrange("p t m -> p m t"),
                 1.0, 0.0, MULT, ADD,
             )
-        gather(3, 0, E)
+        gather(3, 0, B)
         interleave(g23, 2, 0)
-        gather(3, E, E)
+        gather(3, B, B)
         interleave(g23, 2, 1)
-        for q in range(12):
+        for q in range(14):
             c = q % 8 * 32
             nc.tensor.transpose(
                 turned[:, q % 4, :], xb[0][:, c : c + 32, :].rearrange("p n t -> p (n t)"), ident[:]
             )
-        gather(3, 2 * E, E)
+        gather(3, 2 * B, B)
         interleave(g23, 2, 2)
+        gather(3, 3 * B, B)
+        interleave(g23, 2, 3)
         quantise(0)
         nc.vector.quantize_mx(
             out=w_codes[:].bitcast(FP8X4), scales=w_scales[:], in_=wb[:].rearrange("p m t -> p (m t)")
         )
-        multiply(0)
-        gather(3, 3 * E, E)
-        interleave(g23, 2, 3)
-        interleave(g23, 2, 4)
+        acc00 = multiply(0, 0)
+        acc01 = multiply(0, 1)
         quantise(1)
-        multiply(1)
-        reduce(0)
-        quantise(2)
-        multiply(2)
-        reduce(1)
-        finish(0, 128)
-        quantise(3)
-        multiply(3)
-        reduce(2)
-        quantise(4)
-        multiply(4)
-        reduce(3)
-        reduce(4)
-        finish(128, 128)
+        finish(0, 0, acc00)
+        acc10 = multiply(1, 0)
+        acc11 = multiply(1, 1)
+        finish(0, 1, acc01)
+        finish(1, 0, acc10)
+        finish(1, 1, acc11)

@@ -1,7 +1,6 @@
 from contextlib import ExitStack
 
 import concourse.mybir as mybir
-from concourse.masks import make_identity
 
 G, K, T, D, M = 256, 4, 2048, 512, 256
 FLOPS = 2 * D * M * G * K
@@ -53,8 +52,6 @@ def tile_attend_edge_relu_kernel(tc, xT, w, bias, offs, out):
         warm = keep.tile([P, 1], F32, name="warm")
         nc.gpsimd.memset(warm[:], 0.0)
         nc.scalar.activation(warm[:], warm[:], RELU)
-        ident = keep.tile([P, P], BF16, name="ident")
-        make_identity(nc, ident[:])
 
         g01 = keep.tile([P, 2, G * K], F32, name="g01", align_bytes=64)
         g23 = keep.tile([P, 2, G * K], F32, name="g23", align_bytes=64)
@@ -64,7 +61,6 @@ def tile_attend_edge_relu_kernel(tc, xT, w, bias, offs, out):
         wb = keep.tile([P, M, PACK], BF16, name="wb", align_bytes=64)
         w_codes = keep.tile([P, M], U32, name="w_codes", align_bytes=64)
         w_scales = keep.tile([P, M], U8, name="w_scales", align_bytes=64)
-        turned = psum.tile([P, 4, P], BF16, name="turned")
 
         def gather(t, first, count):
             dst = g01 if t < 2 else g23
@@ -125,11 +121,6 @@ def tile_attend_edge_relu_kernel(tc, xT, w, bias, offs, out):
         interleave(g23, 2, 0)
         gather(3, B, B)
         interleave(g23, 2, 1)
-        for q in range(14):
-            c = q % 8 * 32
-            nc.tensor.transpose(
-                turned[:, q % 4, :], xb[0][:, c : c + 32, :].rearrange("p n t -> p (n t)"), ident[:]
-            )
         gather(3, 2 * B, B)
         interleave(g23, 2, 2)
         gather(3, 3 * B, B)

from contextlib import ExitStack

import concourse.mybir as mybir

G, K, T, D, M = 256, 4, 2048, 512, 256
FLOPS = 2 * D * M * G * K

P = 128
PACK = 4
NH = 2
HE = G * K // NH
HG = G // NH
B = 256
MB = M // P

F32 = mybir.dt.float32
BF16 = mybir.dt.bfloat16
U32 = mybir.dt.uint32
U16 = mybir.dt.uint16
U8 = mybir.dt.uint8
FP8X4 = mybir.dt.float8_e4m3fn_x4
MAX = mybir.AluOpType.max
MULT = mybir.AluOpType.mult
ADD = mybir.AluOpType.add
RELU = mybir.ActivationFunctionType.Relu
X = mybir.AxisListType.X


def tile_attend_edge_relu_kernel(tc, xT, w, bias, offs, out):
    nc = tc.nc
    with ExitStack() as ctx:
        keep = ctx.enter_context(tc.tile_pool(name="keep", bufs=1))
        psum = ctx.enter_context(tc.psum_pool(name="psum", bufs=1))

        offsets = keep.tile([P, G * K // 16], U16, name="offsets")
        nc.sync.dma_start(offsets[:], offs)

        x_rows = xT.rearrange("(p t) c -> p t c", t=PACK)
        planes = []
        for t in range(PACK):
            plane = keep.tile([P, T], F32, name="plane%d" % t, align_bytes=64)
            nc.sync.dma_start(plane[:], x_rows[:, t, :])
            planes.append(plane)
        w_raw = keep.tile([P, PACK, M], F32, name="w_raw", align_bytes=64)
        nc.sync.dma_start(w_raw[:], w.rearrange("(p t) m -> p t m", t=PACK))
        bias_sb = []
        for m in range(MB):
            b = keep.tile([P, 1], F32, name="bias%d" % m)
            nc.sync.dma_start(b[:], bias[m * P : (m + 1) * P, :])
            bias_sb.append(b)

        warm = keep.tile([P, 1], F32, name="warm")
        nc.gpsimd.memset(warm[:], 0.0)
        nc.scalar.activation(warm[:], warm[:], RELU)

        g01 = keep.tile([P, 2, G * K], F32, name="g01", align_bytes=64)
        g23 = keep.tile([P, 2, G * K], F32, name="g23", align_bytes=64)
        xb = [keep.tile([P, HE, PACK], BF16, name="xb%d" % h, align_bytes=64) for h in range(NH)]
        codes = [keep.tile([P, HE], U32, name="codes%d" % h, align_bytes=64) for h in range(NH)]
        scales = [keep.tile([P, HE], U8, name="scales%d" % h, align_bytes=64) for h in range(NH)]
        wb = keep.tile([P, M, PACK], BF16, name="wb", align_bytes=64)
        w_codes = keep.tile([P, M], U32, name="w_codes", align_bytes=64)
        w_scales = keep.tile([P, M], U8, name="w_scales", align_bytes=64)

        def gather(t, first, count):
            dst = g01 if t < 2 else g23
            nc.vector.tensor_copy(
                dst[:, t % 2, first : first + count],
                planes[t][:].indirect(offsets[:, first // 16 : (first + count) // 16]),
            )

        def interleave(src, t0, s):
            h, c = divmod(s * B, HE)
            nc.scalar.copy(
                xb[h][:, c : c + B, t0 : t0 + 2],
                src[:, :, s * B : (s + 1) * B].rearrange("p t n -> p n t"),
            )

        def quantise(h):
            nc.vector.quantize_mx(
                out=codes[h][:].bitcast(FP8X4),
                scales=scales[h][:],
                in_=xb[h][:].rearrange("p n t -> p (n t)"),
            )

        def multiply(h, m):
            acc = psum.tile([P, HE], F32, name="acc%d%d" % (h, m))
            nc.tensor.matmul_mx(
                out=acc[:],
                lhsT=w_codes[:, m * P : (m + 1) * P].bitcast(FP8X4),
                lhsT_scale=w_scales[:, m * P : (m + 1) * P],
                rhs=codes[h][:].bitcast(FP8X4),
                rhs_scale=scales[h][:],
                start=True,
                stop=True,
            )
            return acc

        def finish(h, m, acc):
            best = keep.tile([P, HG], F32, name="best%d%d" % (h, m))
            res = keep.tile([P, HG], F32, name="res%d%d" % (h, m))
            nc.vector.tensor_reduce(
                out=best[:], in_=acc[:].rearrange("p (g j) -> p g j", j=K), axis=X, op=MAX
            )
            nc.scalar.activation(res[:], best[:], RELU, bias=bias_sb[m][:, 0:1])
            nc.sync.dma_start(out[m * P : (m + 1) * P, h * HG : (h + 1) * HG], res[:])

        for t in range(3):
            for h in range(NH):
                gather(t, h * HE, HE)
            if t == 1:
                for s in range(4):
                    interleave(g01, 0, s)
        for q in range(4):
            nc.gpsimd.tensor_scalar(
                wb[:, q * 64 : (q + 1) * 64, :],
                w_raw[:, :, q * 64 : (q + 1) * 64].rearrange("p t m -> p m t"),
                1.0, 0.0, MULT, ADD,
            )
        gather(3, 0, B)
        interleave(g23, 2, 0)
        gather(3, B, B)
        interleave(g23, 2, 1)
        gather(3, 2 * B, B)
        interleave(g23, 2, 2)
        gather(3, 3 * B, B)
        interleave(g23, 2, 3)
        quantise(0)
        nc.vector.quantize_mx(
            out=w_codes[:].bitcast(FP8X4), scales=w_scales[:], in_=wb[:].rearrange("p m t -> p (m t)")
        )
        acc00 = multiply(0, 0)
        acc01 = multiply(0, 1)
        quantise(1)
        finish(0, 0, acc00)
        acc10 = multiply(1, 0)
        acc11 = multiply(1, 1)
        finish(0, 1, acc01)
        finish(1, 0, acc10)
        finish(1, 1, acc11)
